import numpy as np
import ml_dtypes


def mxq(x, axis, fmt="e4m3"):
    dtype, down = {"e4m3": (ml_dtypes.float8_e4m3fn, 7), "e5m2": (ml_dtypes.float8_e5m2, 14)}[fmt]
    v = np.moveaxis(np.asarray(x, np.float32).astype(ml_dtypes.bfloat16).astype(np.float64), axis, -1)
    blocks = v.reshape(v.shape[:-1] + (-1, 32))
    amax = np.abs(blocks).max(-1, keepdims=True)
    byte = np.maximum(np.where(amax > 0, np.frexp(amax)[1] - 1 + 127, 0) - down, 1)
    scale = np.exp2(byte - 127.0)
    codes = (blocks / scale).astype(np.float32).astype(dtype).astype(np.float64)
    return np.moveaxis((codes * scale).reshape(v.shape), -1, axis)


WIDE = False


def mx_kscale(k):
    if not WIDE:
        return np.ones(k)
    levels = np.array([10, -10, 5, -5, 0])
    if k % 512:
        return np.exp2(np.random.permutation(np.resize(levels, k // 32))).repeat(32)
    a = np.empty((k // 512, 16))
    for p in range(k // 512):
        a[p, :8] = np.random.permutation(np.resize(levels, 8))
        for g in range(8):
            far = levels[np.abs(levels - a[p, g]) >= 10]
            a[p, g + 8] = far[np.random.randint(len(far))]
    return np.exp2(a.ravel()).repeat(32)


def f64(x):
    return np.asarray(x).astype(np.float64)


def striped(idx):
    return np.tile(idx.reshape(-1, 16).T, (8, 1)).astype(np.uint16)


def unstriped(offs):
    return offs[:16].T.reshape(-1).astype(np.int64)


def pack_weight(w):
    k, n = w.shape
    w = f64(np.asarray(w, np.float32).astype(ml_dtypes.bfloat16)).reshape(k // 32, 32, n)
    amax = np.abs(w).max(1)
    byte = np.clip(np.where(amax > 0, np.frexp(amax)[1] - 1 + 127 - 7, 1), 1, 254)
    scaled = (w * np.exp2(127.0 - byte)[:, None, :]).reshape(k, n).astype(np.float32)
    words = np.ascontiguousarray(scaled.reshape(k // 512, 128, 4, n).transpose(0, 1, 3, 2)).astype(ml_dtypes.float8_e4m3fn).view(np.uint8)
    return words, np.ascontiguousarray(byte.astype(np.uint8).reshape(k // 512, 16, n))


def unpack_weight(words, scales):
    g, p, n, _ = words.shape
    vals = np.ascontiguousarray(words).view(ml_dtypes.float8_e4m3fn).astype(np.float64) * np.repeat(np.exp2(scales.astype(np.float64) - 127.0), 8, axis=1)[..., None]
    return vals.transpose(0, 1, 3, 2).reshape(g * 512, n)


def sigmoid(v):
    return 1.0 / (1.0 + np.exp(-np.maximum(v, -700.0)))


K, T, S, D, H, N = 512, 1024, 512, 4, 512, 128
P = 2 ** 7


def setup_inputs():
    n = np.random.standard_normal
    s = mx_kscale(K)[:, None]
    u = mx_kscale(H)
    packed_xT = pack_weight(n((K, T)) * s)
    packed_eT = pack_weight(n((K, T)) * s)
    packed_dT = pack_weight(n((K, T)) * s)
    return {
        "x_words": packed_xT[0],
        "x_scales": packed_xT[1],
        "e_words": packed_eT[0],
        "e_scales": packed_eT[1],
        "d_words": packed_dT[0],
        "d_scales": packed_dT[1],
        "w1": (n((K, H)) / np.sqrt(K) / s * u).astype(np.float32),
        "bl0": (np.tile(np.random.uniform(0.2, 0.8, S), (P, 1))).astype(np.float32),
        "w2": (n((K, H)) / np.sqrt(K) / s).astype(np.float32),
        "bl1": (np.tile(np.random.uniform(0.2, 0.8, S), (P, 1))).astype(np.float32),
        "w3": (n((K, H)) / np.sqrt(K) / s).astype(np.float32),
        "bl2": (np.tile(np.random.uniform(0.2, 0.8, S), (P, 1))).astype(np.float32),
        "w4": (n((H, N)) / np.sqrt(H) / u[:, None]).astype(np.float32),
        "offs": striped(np.random.permutation(T)[:S]),
        "plb": striped(np.random.permutation(T)[:S]),
        "plc": striped(np.random.permutation(T)[:S]),
    }


def reference(x_words, x_scales, e_words, e_scales, d_words, d_scales, w1, bl0, w2, bl1, w3, bl2, w4, offs, plb, plc):
    xq = unpack_weight(x_words, x_scales)[:, unstriped(offs)]
    y0 = ((mxq(f64(w1), 0, "e4m3").T @ xq)) * f64(bl0)[:1]
    f0 = y0.reshape(len(y0), -1, D).sum(axis=2)
    e_plb = unpack_weight(e_words, e_scales)[:, unstriped(plb)]
    y1 = ((mxq(f64(w2), 0, "e4m3").T @ e_plb)) * f64(bl1)[:1]
    f1 = y1.reshape(len(y1), -1, D).sum(axis=2)
    d_plc = unpack_weight(d_words, d_scales)[:, unstriped(plc)]
    y2 = ((mxq(f64(w3), 0, "e4m3").T @ d_plc)) * f64(bl2)[:1]
    f2 = y2.reshape(len(y2), -1, D).sum(axis=2)
    z = (f0 * f1) * f2
    return sigmoid(mxq(f64(w4), 0, "e4m3").T @ mxq(z, 0, "e4m3"))

@@ -1,0 +1,205 @@
+from contextlib import ExitStack
+
+import concourse.mybir as mybir
+from concourse.masks import make_identity
+
+K, T, S, D, H, N = 512, 1024, 512, 4, 512, 128
+FLOPS = 2 * (3 * K * H * S + H * N * (S // D))
+
+F32 = mybir.dt.float32
+BF16 = mybir.dt.bfloat16
+I32 = mybir.dt.int32
+U32 = mybir.dt.uint32
+U16 = mybir.dt.uint16
+U8 = mybir.dt.uint8
+FP8X4 = mybir.dt.float8_e4m3fn_x4
+COPY = mybir.ActivationFunctionType.Copy
+SIGMOID = mybir.ActivationFunctionType.Sigmoid
+MULT = mybir.AluOpType.mult
+ADD = mybir.AluOpType.add
+
+P = 128
+PACK = 4
+V = S // D
+HALF = H // 2
+
+
+def tile_picked_ytripl_sigmoid_p_kernel(
+    tc, x_words, x_scales, e_words, e_scales, d_words, d_scales, w1, bl0, w2, bl1, w3, bl2, w4, offs, plb, plc, out
+):
+    nc = tc.nc
+    words_in = (x_words, e_words, d_words)
+    scales_in = (x_scales, e_scales, d_scales)
+    lists_in = (offs, plb, plc)
+    weights_in = (w1, w2, w3)
+    bl_in = (bl0, bl1, bl2)
+
+    with ExitStack() as ctx:
+        keep = ctx.enter_context(tc.tile_pool(name="keep", bufs=1))
+        psum = ctx.enter_context(tc.psum_pool(name="psum", bufs=1))
+        ring = ctx.enter_context(tc.psum_pool(name="ring", bufs=4))
+
+        def sb(shape, dtype, name):
+            return keep.tile(shape, dtype, name=name, align_bytes=64)
+
+        lists = [sb([P, S // 16], U16, "list%d" % s) for s in range(3)]
+        word_win = [sb([P, T], I32, "wordwin%d" % s) for s in range(3)]
+        scale_win = [sb([P, T], U8, "scalewin%d" % s) for s in range(3)]
+        bl = [sb([P, D], F32, "bl%d" % s) for s in range(3)]
+        w_raw = [sb([P, PACK, H], F32, "wraw%d" % s) for s in range(2)]
+        w3_raw = [sb([P, PACK, HALF], F32, "w3raw%d" % h) for h in range(2)]
+        w4_raw = sb([P, PACK, N], F32, "w4raw")
+        ident = sb([P, P], F32, "ident")
+
+        for s in range(3):
+            nc.vector.memset(scale_win[s][:].bitcast(I32), 0)
+        make_identity(nc, ident[:])
+
+        def load_scales(s):
+            nc.sync.dma_start(lists[s][:], lists_in[s])
+            for q in range(4):
+                nc.sync.dma_start(
+                    scale_win[s][32 * q : 32 * q + 4, :].bitcast(I32), scales_in[s][0, 4 * q : 4 * q + 4, :].bitcast(I32)
+                )
+
+        def load_words(s):
+            nc.sync.dma_start(word_win[s][:], words_in[s][0].rearrange("p n t -> p (n t)").bitcast(I32))
+
+        def rows(w):
+            return w.rearrange("(p j) c -> p j c", j=PACK)
+
+        def load_bl(s):
+            nc.sync.dma_start(bl[s][:], bl_in[s][0].rearrange("(v d) -> v d", d=D))
+
+        warm = sb([P, 1], F32, "warm")
+        nc.vector.memset(warm[:], 0.0)
+        nc.scalar.activation(warm[:], warm[:], SIGMOID)
+        nc.sync.dma_start(w_raw[0][:], rows(w1))
+        load_scales(0)
+        load_words(0)
+        load_bl(0)
+        load_scales(1)
+        nc.sync.dma_start(w_raw[1][:], rows(w2))
+        load_words(1)
+        load_bl(1)
+        load_scales(2)
+        load_words(2)
+        load_bl(2)
+        for h in range(2):
+            nc.sync.dma_start(w3_raw[h][:], rows(w3)[:, :, h * HALF : (h + 1) * HALF])
+        nc.sync.dma_start(w4_raw[:], rows(w4))
+
+        tok_words = [sb([P, D, V], U32, "tokw%d" % s) for s in range(3)]
+        tok_bytes = [sb([P, S], U8, "tokb%d" % s) for s in range(3)]
+        tok_scales = [sb([P, D, V], U8, "toks%d" % s) for s in range(3)]
+
+        def gather_scales(s):
+            nc.vector.tensor_copy(tok_bytes[s][:], scale_win[s][:].indirect(lists[s][:]))
+
+        def deal_scales(s):
+            nc.vector.tensor_copy(tok_scales[s][:], tok_bytes[s][:].rearrange("p (v d) -> p d v", d=D))
+
+        def gather_words(s):
+            nc.vector.tensor_copy(tok_words[s][:].rearrange("p d v -> p v d"), word_win[s][:].bitcast(U32).indirect(lists[s][:]))
+
+        def cast(on_scalar, grouped, raw):
+            dst = grouped.rearrange("p (c i) j -> p c j i", i=4)
+            src = raw.rearrange("p j (c i) -> p c j i", i=4)
+            if on_scalar:
+                nc.scalar.copy(dst, src)
+            else:
+                nc.vector.tensor_copy(dst, src)
+
+        def quantize(codes, scales, grouped):
+            nc.vector.quantize_mx(out=codes.bitcast(FP8X4), scales=scales, in_=grouped.rearrange("p c j -> p (c j)"))
+
+        w_grp = [sb([P, H, PACK], BF16, "wgrp%d" % s) for s in range(3)]
+        w_codes = [sb([P, H], U32, "wcodes%d" % s) for s in range(3)]
+        w_scales = [sb([P, H], U8, "wscales%d" % s) for s in range(3)]
+        w4_grp = sb([P, N, PACK], BF16, "w4grp")
+        w4_codes = sb([P, N], U32, "w4codes")
+        w4_scales = sb([P, N], U8, "w4scales")
+
+        def product(s, d, c0, n):
+            y = ring.tile([P, n], F32, name="y", tag="y")
+            nc.tensor.matmul_mx(
+                out=y[:],
+                lhsT=tok_words[s][:, d, :].bitcast(FP8X4),
+                lhsT_scale=tok_scales[s][:, d, :],
+                rhs=w_codes[s][:, c0 : c0 + n].bitcast(FP8X4),
+                rhs_scale=w_scales[s][:, c0 : c0 + n],
+                start=True,
+                stop=True,
+            )
+            return y[:].rearrange("v (m t) -> v t m", t=PACK)
+
+        def turn(f, terms):
+            for a, term in enumerate(terms):
+                for t in range(PACK):
+                    nc.tensor.matmul(
+                        f[:, t, :], term[:, t, :], ident[:], is_transpose=True,
+                        start=(a == 0 and t == 0), stop=(a == len(terms) - 1 and t == PACK - 1),
+                    )
+
+        feat = [psum.tile([P, PACK, V], F32, name="feat%d" % s) for s in range(3)]
+        scaled = [[sb([P, PACK, P], F32, "scaled%d_%d" % (s, d)) for d in range(D)] for s in range(3)]
+
+        def full_table(s):
+            for d in range(D):
+                y = product(s, d, 0, H)
+                nc.scalar.activation(scaled[s][d][:], y, COPY, scale=bl[s][:, d : d + 1])
+            turn(feat[s], scaled[s])
+
+        gather_scales(0)
+        cast(False, w_grp[0][:, :HALF, :], w_raw[0][:, :, :HALF])
+        cast(True, w_grp[0][:, HALF:, :], w_raw[0][:, :, HALF:])
+        deal_scales(0)
+        gather_words(0)
+        quantize(w_codes[0][:], w_scales[0][:], w_grp[0][:])
+        gather_scales(1)
+        full_table(0)
+        deal_scales(1)
+        cast(True, w_grp[1][:, :HALF, :], w_raw[1][:, :, :HALF])
+        cast(True, w_grp[1][:, HALF:, :], w_raw[1][:, :, HALF:])
+        gather_words(1)
+        gather_scales(2)
+        quantize(w_codes[1][:], w_scales[1][:], w_grp[1][:])
+        deal_scales(2)
+        full_table(1)
+        gather_words(2)
+        f0 = sb([P, V, PACK], F32, "f0")
+        nc.scalar.copy(f0[:], feat[0][:].rearrange("p t v -> p v t"))
+
+        pair = [sb([P, PACK, P], F32, "pair%d" % a) for a in range(2)]
+        for h in range(2):
+            cols = slice(h * HALF, (h + 1) * HALF)
+            cast(False, w_grp[2][:, cols, :], w3_raw[h][:])
+            quantize(w_codes[2][:, cols], w_scales[2][:, cols], w_grp[2][:, cols, :])
+        for h in range(2):
+            part = slice(h * P // 2, (h + 1) * P // 2)
+            for a in range(2):
+                y = product(2, 2 * a, h * HALF, HALF)
+                nc.scalar.activation(scaled[2][2 * a][:, :, part], y, COPY, scale=bl[2][:, 2 * a : 2 * a + 1])
+                y = product(2, 2 * a + 1, h * HALF, HALF)
+                nc.vector.scalar_tensor_tensor(
+                    pair[a][:, :, part], y, bl[2][:, 2 * a + 1 : 2 * a + 2], scaled[2][2 * a][:, :, part], MULT, ADD
+                )
+        cast(True, w4_grp[:], w4_raw[:])
+        f01 = sb([P, V, PACK], F32, "f01")
+        nc.vector.tensor_tensor(f01[:], feat[1][:].rearrange("p t v -> p v t"), f0[:], MULT)
+        quantize(w4_codes[:], w4_scales[:], w4_grp[:])
+        turn(feat[2], pair)
+
+        z = sb([P, V, PACK], BF16, "z")
+        z_codes = sb([P, V], U32, "zcodes")
+        z_scales = sb([P, V], U8, "zscales")
+        nc.vector.tensor_tensor(z[:], feat[2][:].rearrange("p t v -> p v t"), f01[:], MULT)
+        quantize(z_codes[:], z_scales[:], z[:])
+        acc = psum.tile([P, V], F32, name="acc")
+        nc.tensor.matmul_mx(
+            out=acc[:], lhsT=w4_codes[:].bitcast(FP8X4), lhsT_scale=w4_scales[:],
+            rhs=z_codes[:].bitcast(FP8X4), rhs_scale=z_scales[:], start=True, stop=True,
+        )
+        result = sb([P, V], F32, "result")
+        nc.scalar.activation(result[:], acc[:], SIGMOID)
+        nc.sync.dma_start(out, result[:])

@@ -46,19 +46,17 @@ def tile_picked_ytripl_sigmoid_p_kernel(
         word_win = [sb([P, T], I32, "wordwin%d" % s) for s in range(3)]
         scale_win = [sb([P, T], U8, "scalewin%d" % s) for s in range(3)]
         bl = [sb([P, D], F32, "bl%d" % s) for s in range(3)]
-        w_raw = [sb([P, PACK, H], F32, "wraw%d" % s) for s in range(2)]
-        w3_raw = [sb([P, PACK, HALF], F32, "w3raw%d" % h) for h in range(2)]
+        loads = [[[0,256],[256,256]],[[0,256],[256,256]],[[0,256],[256,256]]]
+        w_raw = [[sb([P, PACK, n], F32, "wraw%d_%d" % (s, c0)) for c0, n in loads[s]] for s in range(3)]
         w4_raw = sb([P, PACK, N], F32, "w4raw")
         ident = sb([P, P], F32, "ident")
 
-        for s in range(3):
-            nc.vector.memset(scale_win[s][:].bitcast(I32), 0)
-        make_identity(nc, ident[:])
-
-        def load_scales(s):
+        def load_list(s):
             nc.sync.dma_start(lists[s][:], lists_in[s])
+
+        def load_scales(s, eng=nc.sync):
             for q in range(4):
-                nc.sync.dma_start(
+                eng.dma_start(
                     scale_win[s][32 * q : 32 * q + 4, :].bitcast(I32), scales_in[s][0, 4 * q : 4 * q + 4, :].bitcast(I32)
                 )
 
@@ -68,25 +66,39 @@ def tile_picked_ytripl_sigmoid_p_kernel(
         def rows(w):
             return w.rearrange("(p j) c -> p j c", j=PACK)
 
-        def load_bl(s):
-            nc.sync.dma_start(bl[s][:], bl_in[s][0].rearrange("(v d) -> v d", d=D))
+        def load_w(s, a):
+            c0, n = loads[s][a]
+            nc.sync.dma_start(w_raw[s][a][:], rows(weights_in[s])[:, :, c0 : c0 + n])
+
+        def load_bl(s, eng):
+            eng.dma_start(bl[s][:], bl_in[s][0].rearrange("(v d) -> v d", d=D))
 
         warm = sb([P, 1], F32, "warm")
         nc.vector.memset(warm[:], 0.0)
         nc.scalar.activation(warm[:], warm[:], SIGMOID)
-        nc.sync.dma_start(w_raw[0][:], rows(w1))
+
+        nc.gpsimd.memset(scale_win[0][:].bitcast(I32), 0)
+        nc.gpsimd.memset(scale_win[1][:].bitcast(I32), 0)
+        nc.gpsimd.memset(scale_win[2][:].bitcast(I32), 0)
+        load_bl(0, nc.gpsimd)
+        make_identity(nc, ident[:])
+        load_bl(1, nc.gpsimd)
+        load_bl(2, nc.gpsimd)
+        load_list(0)
         load_scales(0)
         load_words(0)
-        load_bl(0)
+        load_w(0,0)
+        load_list(1)
         load_scales(1)
-        nc.sync.dma_start(w_raw[1][:], rows(w2))
+        load_w(0,1)
+        load_w(1,0)
         load_words(1)
-        load_bl(1)
-        load_scales(2)
+        load_w(1,1)
         load_words(2)
-        load_bl(2)
-        for h in range(2):
-            nc.sync.dma_start(w3_raw[h][:], rows(w3)[:, :, h * HALF : (h + 1) * HALF])
+        load_list(2)
+        load_scales(2)
+        load_w(2,0)
+        load_w(2,1)
         nc.sync.dma_start(w4_raw[:], rows(w4))
 
         tok_words = [sb([P, D, V], U32, "tokw%d" % s) for s in range(3)]
@@ -102,13 +114,15 @@ def tile_picked_ytripl_sigmoid_p_kernel(
         def gather_words(s):
             nc.vector.tensor_copy(tok_words[s][:].rearrange("p d v -> p v d"), word_win[s][:].bitcast(U32).indirect(lists[s][:]))
 
-        def cast(on_scalar, grouped, raw):
+        def cast(eng, grouped, raw):
             dst = grouped.rearrange("p (c i) j -> p c j i", i=4)
             src = raw.rearrange("p j (c i) -> p c j i", i=4)
-            if on_scalar:
+            if eng == "S":
                 nc.scalar.copy(dst, src)
-            else:
+            elif eng == "V":
                 nc.vector.tensor_copy(dst, src)
+            else:
+                nc.gpsimd.tensor_copy(dst, src)
 
         def quantize(codes, scales, grouped):
             nc.vector.quantize_mx(out=codes.bitcast(FP8X4), scales=scales, in_=grouped.rearrange("p c j -> p (c j)"))
@@ -119,6 +133,14 @@ def tile_picked_ytripl_sigmoid_p_kernel(
         w4_grp = sb([P, N, PACK], BF16, "w4grp")
         w4_codes = sb([P, N], U32, "w4codes")
         w4_scales = sb([P, N], U8, "w4scales")
+
+        def cast_w(eng, s, c0, n):
+            for a, (l0, ln) in enumerate(loads[s]):
+                if l0 <= c0 and c0 + n <= l0 + ln:
+                    cast(eng, w_grp[s][:, c0 : c0 + n, :], w_raw[s][a][:, :, c0 - l0 : c0 - l0 + n])
+
+        def quant_w(s, c0, n):
+            quantize(w_codes[s][:, c0 : c0 + n], w_scales[s][:, c0 : c0 + n], w_grp[s][:, c0 : c0 + n, :])
 
         def product(s, d, c0, n):
             y = ring.tile([P, n], F32, name="y", tag="y")
@@ -143,52 +165,57 @@ def tile_picked_ytripl_sigmoid_p_kernel(
 
         feat = [psum.tile([P, PACK, V], F32, name="feat%d" % s) for s in range(3)]
         scaled = [[sb([P, PACK, P], F32, "scaled%d_%d" % (s, d)) for d in range(D)] for s in range(3)]
+        pair = [[sb([P, PACK, P], F32, "pair%d_%d" % (s, a)) for a in range(2)] for s in range(3)]
 
-        def full_table(s):
+        def products(s, c0, n, engs="SSSS"):
+            part = slice(c0 // PACK, (c0 + n) // PACK)
             for d in range(D):
-                y = product(s, d, 0, H)
-                nc.scalar.activation(scaled[s][d][:], y, COPY, scale=bl[s][:, d : d + 1])
-            turn(feat[s], scaled[s])
+                y = product(s, d, c0, n)
+                if engs[d] == "S":
+                    nc.scalar.activation(scaled[s][d][:, :, part], y, COPY, scale=bl[s][:, d : d + 1])
+                elif engs[d] == "V":
+                    nc.vector.tensor_scalar(scaled[s][d][:, :, part], y, bl[s][:, d : d + 1], None, MULT)
+                else:
+                    nc.vector.scalar_tensor_tensor(
+                        pair[s][d // 2][:, :, part], y, bl[s][:, d : d + 1], scaled[s][d - 1][:, :, part], MULT, ADD
+                    )
+
+        f0 = sb([P, V, PACK], F32, "f0")
+        f01 = sb([P, V, PACK], F32, "f01")
 
         gather_scales(0)
-        cast(False, w_grp[0][:, :HALF, :], w_raw[0][:, :, :HALF])
-        cast(True, w_grp[0][:, HALF:, :], w_raw[0][:, :, HALF:])
         deal_scales(0)
         gather_words(0)
-        quantize(w_codes[0][:], w_scales[0][:], w_grp[0][:])
+        cast_w("V", 0, 0, 256)
+        cast_w("S", 0, 256, 256)
+        quant_w(0, 0, 256)
+        quant_w(0, 256, 256)
         gather_scales(1)
-        full_table(0)
         deal_scales(1)
-        cast(True, w_grp[1][:, :HALF, :], w_raw[1][:, :, :HALF])
-        cast(True, w_grp[1][:, HALF:, :], w_raw[1][:, :, HALF:])
+        cast_w("S", 1, 0, 256)
+        products(0, 0, 256)
+        products(0, 256, 256)
         gather_words(1)
+        cast_w("V", 1, 256, 256)
+        quant_w(1, 0, 256)
+        quant_w(1, 256, 256)
         gather_scales(2)
-        quantize(w_codes[1][:], w_scales[1][:], w_grp[1][:])
-        deal_scales(2)
-        full_table(1)
         gather_words(2)
-        f0 = sb([P, V, PACK], F32, "f0")
+        deal_scales(2)
+        products(1, 0, 256)
+        cast_w("S", 2, 0, 256)
+        products(1, 256, 256)
+        cast_w("V", 2, 256, 256)
+        quant_w(2, 0, 256)
+        quant_w(2, 256, 256)
+        turn(feat[0], scaled[0])
         nc.scalar.copy(f0[:], feat[0][:].rearrange("p t v -> p v t"))
-
-        pair = [sb([P, PACK, P], F32, "pair%d" % a) for a in range(2)]
-        for h in range(2):
-            cols = slice(h * HALF, (h + 1) * HALF)
-            cast(False, w_grp[2][:, cols, :], w3_raw[h][:])
-            quantize(w_codes[2][:, cols], w_scales[2][:, cols], w_grp[2][:, cols, :])
-        for h in range(2):
-            part = slice(h * P // 2, (h + 1) * P // 2)
-            for a in range(2):
-                y = product(2, 2 * a, h * HALF, HALF)
-                nc.scalar.activation(scaled[2][2 * a][:, :, part], y, COPY, scale=bl[2][:, 2 * a : 2 * a + 1])
-                y = product(2, 2 * a + 1, h * HALF, HALF)
-                nc.vector.scalar_tensor_tensor(
-                    pair[a][:, :, part], y, bl[2][:, 2 * a + 1 : 2 * a + 2], scaled[2][2 * a][:, :, part], MULT, ADD
-                )
-        cast(True, w4_grp[:], w4_raw[:])
-        f01 = sb([P, V, PACK], F32, "f01")
+        turn(feat[1], scaled[1])
+        cast("S", w4_grp[:], w4_raw[:])
         nc.vector.tensor_tensor(f01[:], feat[1][:].rearrange("p t v -> p v t"), f0[:], MULT)
         quantize(w4_codes[:], w4_scales[:], w4_grp[:])
-        turn(feat[2], pair)
+        products(2, 0, 512, "SVSV")
+        turn(feat[2], scaled[2])
 
         z = sb([P, V, PACK], BF16, "z")
         z_codes = sb([P, V], U32, "zcodes")

@@ -81,8 +81,8 @@ def tile_picked_ytripl_sigmoid_p_kernel(
         nc.gpsimd.memset(scale_win[1][:].bitcast(I32), 0)
         nc.gpsimd.memset(scale_win[2][:].bitcast(I32), 0)
         load_bl(0, nc.gpsimd)
-        make_identity(nc, ident[:])
         load_bl(1, nc.gpsimd)
+        make_identity(nc, ident[:])
         load_bl(2, nc.gpsimd)
         load_list(0)
         load_scales(0)
@@ -186,34 +186,29 @@ def tile_picked_ytripl_sigmoid_p_kernel(
         gather_scales(0)
         deal_scales(0)
         gather_words(0)
-        cast_w("V", 0, 0, 256)
+        cast_w("S", 0, 0, 256)
         cast_w("S", 0, 256, 256)
-        quant_w(0, 0, 256)
-        quant_w(0, 256, 256)
         gather_scales(1)
         deal_scales(1)
+        quant_w(0, 0, 512)
         cast_w("S", 1, 0, 256)
-        products(0, 0, 256)
-        products(0, 256, 256)
+        products(0, 0, 512)
         gather_words(1)
         cast_w("V", 1, 256, 256)
-        quant_w(1, 0, 256)
-        quant_w(1, 256, 256)
+        quant_w(1, 0, 512)
+        products(1, 0, 512)
         gather_scales(2)
         gather_words(2)
         deal_scales(2)
-        products(1, 0, 256)
-        cast_w("S", 2, 0, 256)
-        products(1, 256, 256)
+        cast_w("V", 2, 0, 256)
         cast_w("V", 2, 256, 256)
-        quant_w(2, 0, 256)
-        quant_w(2, 256, 256)
+        quant_w(2, 0, 512)
         turn(feat[0], scaled[0])
         nc.scalar.copy(f0[:], feat[0][:].rearrange("p t v -> p v t"))
         turn(feat[1], scaled[1])
         cast("S", w4_grp[:], w4_raw[:])
-        nc.vector.tensor_tensor(f01[:], feat[1][:].rearrange("p t v -> p v t"), f0[:], MULT)
         quantize(w4_codes[:], w4_scales[:], w4_grp[:])
+        nc.vector.tensor_tensor(f01[:], feat[1][:].rearrange("p t v -> p v t"), f0[:], MULT)
         products(2, 0, 512, "SVSV")
         turn(feat[2], scaled[2])
 

@@ -39,8 +39,8 @@ def tile_picked_ytripl_sigmoid_p_kernel(
         psum = ctx.enter_context(tc.psum_pool(name="psum", bufs=1))
         ring = ctx.enter_context(tc.psum_pool(name="ring", bufs=4))
 
-        def sb(shape, dtype, name):
-            return keep.tile(shape, dtype, name=name, align_bytes=64)
+        def sb(shape, dtype, name, tag=None):
+            return keep.tile(shape, dtype, name=name, tag=tag or name, align_bytes=64)
 
         lists = [sb([P, S // 16], U16, "list%d" % s) for s in range(3)]
         word_win = [sb([P, T], I32, "wordwin%d" % s) for s in range(3)]
@@ -80,10 +80,7 @@ def tile_picked_ytripl_sigmoid_p_kernel(
         nc.gpsimd.memset(scale_win[0][:].bitcast(I32), 0)
         nc.gpsimd.memset(scale_win[1][:].bitcast(I32), 0)
         nc.gpsimd.memset(scale_win[2][:].bitcast(I32), 0)
-        load_bl(0, nc.gpsimd)
-        load_bl(1, nc.gpsimd)
         make_identity(nc, ident[:])
-        load_bl(2, nc.gpsimd)
         load_list(0)
         load_scales(0)
         load_words(0)
@@ -92,14 +89,17 @@ def tile_picked_ytripl_sigmoid_p_kernel(
         load_scales(1)
         load_w(0,1)
         load_w(1,0)
+        load_bl(0, nc.sync)
+        load_bl(1, nc.sync)
         load_words(1)
         load_w(1,1)
-        load_words(2)
         load_list(2)
+        load_words(2)
         load_scales(2)
         load_w(2,0)
         load_w(2,1)
         nc.sync.dma_start(w4_raw[:], rows(w4))
+        load_bl(2, nc.sync)
 
         tok_words = [sb([P, D, V], U32, "tokw%d" % s) for s in range(3)]
         tok_bytes = [sb([P, S], U8, "tokb%d" % s) for s in range(3)]
@@ -181,7 +181,6 @@ def tile_picked_ytripl_sigmoid_p_kernel(
                     )
 
         f0 = sb([P, V, PACK], F32, "f0")
-        f01 = sb([P, V, PACK], F32, "f01")
 
         gather_scales(0)
         deal_scales(0)
@@ -208,6 +207,7 @@ def tile_picked_ytripl_sigmoid_p_kernel(
         turn(feat[1], scaled[1])
         cast("S", w4_grp[:], w4_raw[:])
         quantize(w4_codes[:], w4_scales[:], w4_grp[:])
+        f01 = sb([P, V, PACK], F32, "f01", "wgrp2")
         nc.vector.tensor_tensor(f01[:], feat[1][:].rearrange("p t v -> p v t"), f0[:], MULT)
         products(2, 0, 512, "SVSV")
         turn(feat[2], scaled[2])

@@ -16,212 +16,240 @@ FP8X4 = mybir.dt.float8_e4m3fn_x4
 COPY = mybir.ActivationFunctionType.Copy
 SIGMOID = mybir.ActivationFunctionType.Sigmoid
 MULT = mybir.AluOpType.mult
-ADD = mybir.AluOpType.add
 
 P = 128
-PACK = 4
+SLOTS = 4
+PLANES = 3
+LAST = PLANES - 1
 V = S // D
 HALF = H // 2
+QUADRANT = 32
+RUN = 4
+PRODUCT_BANKS = 5
 
 
 def tile_picked_ytripl_sigmoid_p_kernel(
     tc, x_words, x_scales, e_words, e_scales, d_words, d_scales, w1, bl0, w2, bl1, w3, bl2, w4, offs, plb, plc, out
 ):
     nc = tc.nc
-    words_in = (x_words, e_words, d_words)
-    scales_in = (x_scales, e_scales, d_scales)
-    lists_in = (offs, plb, plc)
-    weights_in = (w1, w2, w3)
-    bl_in = (bl0, bl1, bl2)
+    words_hbm = (x_words, e_words, d_words)
+    scales_hbm = (x_scales, e_scales, d_scales)
+    lists_hbm = (offs, plb, plc)
+    bilinear_hbm = (bl0, bl1, bl2)
+    halves = (slice(0, HALF), slice(HALF, H))
 
     with ExitStack() as ctx:
         keep = ctx.enter_context(tc.tile_pool(name="keep", bufs=1))
-        psum = ctx.enter_context(tc.psum_pool(name="psum", bufs=1))
-        ring = ctx.enter_context(tc.psum_pool(name="ring", bufs=4))
+        feature_banks = ctx.enter_context(tc.psum_pool(name="feature_banks", bufs=1))
+        product_banks = ctx.enter_context(tc.psum_pool(name="product_banks", bufs=PRODUCT_BANKS))
 
-        def sb(shape, dtype, name, tag=None):
+        def sbuf(shape, dtype, name, tag=None):
             return keep.tile(shape, dtype, name=name, tag=tag or name, align_bytes=64)
 
-        lists = [sb([P, S // 16], U16, "list%d" % s) for s in range(3)]
-        word_win = [sb([P, T], I32, "wordwin%d" % s) for s in range(3)]
-        scale_win = [sb([P, T], U8, "scalewin%d" % s) for s in range(3)]
-        bl = [sb([P, D], F32, "bl%d" % s) for s in range(3)]
-        loads = [[[0,256],[256,256]],[[0,256],[256,256]],[[0,256],[256,256]]]
-        w_raw = [[sb([P, PACK, n], F32, "wraw%d_%d" % (s, c0)) for c0, n in loads[s]] for s in range(3)]
-        w4_raw = sb([P, PACK, N], F32, "w4raw")
-        ident = sb([P, P], F32, "ident")
+        def per_plane(shape, dtype, name):
+            return [sbuf(shape, dtype, "%s%d" % (name, s)) for s in range(PLANES)]
+
+        lists = per_plane([P, S // 16], U16, "list")
+        word_table = per_plane([P, T], I32, "word_table")
+        scale_table = per_plane([P, T], U8, "scale_table")
+        bilinear = per_plane([P, D], F32, "bilinear")
+        w_halves = [[sbuf([P, SLOTS, HALF], F32, "w_raw%d_%d" % (s, h)) for h in range(2)] for s in range(LAST)]
+        w3_raw = sbuf([P, SLOTS, H], F32, "w3_raw")
+        w4_raw = sbuf([P, SLOTS, N], F32, "w4_raw")
+        identity = sbuf([P, P], F32, "identity")
 
         def load_list(s):
-            nc.sync.dma_start(lists[s][:], lists_in[s])
+            nc.sync.dma_start(lists[s][:], lists_hbm[s])
 
-        def load_scales(s, eng=nc.sync):
-            for q in range(4):
-                eng.dma_start(
-                    scale_win[s][32 * q : 32 * q + 4, :].bitcast(I32), scales_in[s][0, 4 * q : 4 * q + 4, :].bitcast(I32)
+        def load_scales(s):
+            for q in range(P // QUADRANT):
+                nc.sync.dma_start(
+                    scale_table[s][QUADRANT * q : QUADRANT * q + 4, :].bitcast(I32),
+                    scales_hbm[s][0, 4 * q : 4 * q + 4, :].bitcast(I32),
                 )
 
         def load_words(s):
-            nc.sync.dma_start(word_win[s][:], words_in[s][0].rearrange("p n t -> p (n t)").bitcast(I32))
+            nc.sync.dma_start(word_table[s][:], words_hbm[s][0].rearrange("p c j -> p (c j)").bitcast(I32))
 
-        def rows(w):
-            return w.rearrange("(p j) c -> p j c", j=PACK)
+        def by_slot(w):
+            return w.rearrange("(p j) c -> p j c", j=SLOTS)
 
-        def load_w(s, a):
-            c0, n = loads[s][a]
-            nc.sync.dma_start(w_raw[s][a][:], rows(weights_in[s])[:, :, c0 : c0 + n])
+        def load_weight_half(s, h):
+            nc.sync.dma_start(w_halves[s][h][:], by_slot((w1, w2)[s])[:, :, halves[h]])
 
-        def load_bl(s, eng):
-            eng.dma_start(bl[s][:], bl_in[s][0].rearrange("(v d) -> v d", d=D))
+        def load_bilinear(s):
+            nc.sync.dma_start(bilinear[s][:], bilinear_hbm[s][0].rearrange("(v d) -> v d", d=D))
 
-        warm = sb([P, 1], F32, "warm")
-        nc.vector.memset(warm[:], 0.0)
-        nc.scalar.activation(warm[:], warm[:], SIGMOID)
+        for s in range(PLANES):
+            nc.gpsimd.memset(scale_table[s][:].bitcast(I32), 0)
+        make_identity(nc, identity[:])
 
-        nc.gpsimd.memset(scale_win[0][:].bitcast(I32), 0)
-        nc.gpsimd.memset(scale_win[1][:].bitcast(I32), 0)
-        nc.gpsimd.memset(scale_win[2][:].bitcast(I32), 0)
-        make_identity(nc, ident[:])
         load_list(0)
         load_scales(0)
         load_words(0)
-        load_w(0,0)
+        load_weight_half(0, 0)
         load_list(1)
         load_scales(1)
-        load_w(0,1)
-        load_w(1,0)
-        load_bl(0, nc.sync)
-        load_bl(1, nc.sync)
+        load_weight_half(0, 1)
+        load_weight_half(1, 0)
+        load_bilinear(0)
+        load_bilinear(1)
         load_words(1)
-        load_w(1,1)
-        load_list(2)
-        load_words(2)
-        load_scales(2)
-        load_w(2,0)
-        load_w(2,1)
-        nc.sync.dma_start(w4_raw[:], rows(w4))
-        load_bl(2, nc.sync)
+        load_weight_half(1, 1)
+        load_list(LAST)
+        load_words(LAST)
+        load_scales(LAST)
+        nc.sync.dma_start(w3_raw[:], by_slot(w3))
+        nc.sync.dma_start(w4_raw[:], by_slot(w4))
+        load_bilinear(LAST)
 
-        tok_words = [sb([P, D, V], U32, "tokw%d" % s) for s in range(3)]
-        tok_bytes = [sb([P, S], U8, "tokb%d" % s) for s in range(3)]
-        tok_scales = [sb([P, D, V], U8, "toks%d" % s) for s in range(3)]
-
-        def gather_scales(s):
-            nc.vector.tensor_copy(tok_bytes[s][:], scale_win[s][:].indirect(lists[s][:]))
-
-        def deal_scales(s):
-            nc.vector.tensor_copy(tok_scales[s][:], tok_bytes[s][:].rearrange("p (v d) -> p d v", d=D))
+        picked_words = per_plane([P, D, V], U32, "picked_words")
+        listed_scales = per_plane([P, S], U8, "listed_scales")
+        picked_scales = per_plane([P, D, V], U8, "picked_scales")
 
         def gather_words(s):
-            nc.vector.tensor_copy(tok_words[s][:].rearrange("p d v -> p v d"), word_win[s][:].bitcast(U32).indirect(lists[s][:]))
+            nc.vector.tensor_copy(
+                picked_words[s][:].rearrange("p d v -> p v d"), word_table[s][:].bitcast(U32).indirect(lists[s][:])
+            )
 
-        def cast(eng, grouped, raw):
-            dst = grouped.rearrange("p (c i) j -> p c j i", i=4)
-            src = raw.rearrange("p j (c i) -> p c j i", i=4)
-            if eng == "S":
-                nc.scalar.copy(dst, src)
-            elif eng == "V":
-                nc.vector.tensor_copy(dst, src)
-            else:
-                nc.gpsimd.tensor_copy(dst, src)
+        def gather_scales(s):
+            nc.vector.tensor_copy(listed_scales[s][:], scale_table[s][:].indirect(lists[s][:]))
 
-        def quantize(codes, scales, grouped):
-            nc.vector.quantize_mx(out=codes.bitcast(FP8X4), scales=scales, in_=grouped.rearrange("p c j -> p (c j)"))
+        def deal_scales(s):
+            nc.vector.tensor_copy(picked_scales[s][:], listed_scales[s][:].rearrange("p (v d) -> p d v", d=D))
 
-        w_grp = [sb([P, H, PACK], BF16, "wgrp%d" % s) for s in range(3)]
-        w_codes = [sb([P, H], U32, "wcodes%d" % s) for s in range(3)]
-        w_scales = [sb([P, H], U8, "wscales%d" % s) for s in range(3)]
-        w4_grp = sb([P, N, PACK], BF16, "w4grp")
-        w4_codes = sb([P, N], U32, "w4codes")
-        w4_scales = sb([P, N], U8, "w4scales")
+        w_rounded = per_plane([P, H, SLOTS], BF16, "w_rounded")
+        w_codes = per_plane([P, H], U32, "w_codes")
+        w_scales = per_plane([P, H], U8, "w_scales")
+        w4_rounded = sbuf([P, N, SLOTS], BF16, "w4_rounded")
+        w4_codes = sbuf([P, N], U32, "w4_codes")
+        w4_scales = sbuf([P, N], U8, "w4_scales")
 
-        def cast_w(eng, s, c0, n):
-            for a, (l0, ln) in enumerate(loads[s]):
-                if l0 <= c0 and c0 + n <= l0 + ln:
-                    cast(eng, w_grp[s][:, c0 : c0 + n, :], w_raw[s][a][:, :, c0 - l0 : c0 - l0 + n])
+        def round_columns(copy, rounded, raw):
+            copy(rounded.rearrange("p (c i) j -> p c j i", i=RUN), raw.rearrange("p j (c i) -> p c j i", i=RUN))
 
-        def quant_w(s, c0, n):
-            quantize(w_codes[s][:, c0 : c0 + n], w_scales[s][:, c0 : c0 + n], w_grp[s][:, c0 : c0 + n, :])
+        def round_weight_half(copy, s, h):
+            round_columns(copy, w_rounded[s][:, halves[h], :], w_halves[s][h][:])
 
-        def product(s, d, c0, n):
-            y = ring.tile([P, n], F32, name="y", tag="y")
+        def round_w3_half(h):
+            ts = slice(2 * h, 2 * h + 2)
+            nc.vector.tensor_copy(
+                w_rounded[LAST][:].rearrange("p (t m) j -> p m j t", t=SLOTS)[:, :, :, ts],
+                w3_raw[:].rearrange("p j (m t) -> p m j t", t=SLOTS)[:, :, :, ts],
+            )
+
+        def quantize(codes, scales, rounded):
+            nc.vector.quantize_mx(out=codes.bitcast(FP8X4), scales=scales, in_=rounded.rearrange("p c j -> p (c j)"))
+
+        def quantize_weight(s, cols):
+            quantize(w_codes[s][:, cols], w_scales[s][:, cols], w_rounded[s][:, cols, :])
+
+        feature = [feature_banks.tile([P, SLOTS, V], F32, name="feature%d" % s) for s in range(PLANES)]
+        weighted = [[sbuf([P, SLOTS, P], F32, "weighted%d_%d" % (s, d)) for d in range(D)] for s in range(PLANES)]
+
+        def product(s, d, cols):
+            y = product_banks.tile([P, cols.stop - cols.start], F32, name="y", tag="product")
             nc.tensor.matmul_mx(
                 out=y[:],
-                lhsT=tok_words[s][:, d, :].bitcast(FP8X4),
-                lhsT_scale=tok_scales[s][:, d, :],
-                rhs=w_codes[s][:, c0 : c0 + n].bitcast(FP8X4),
-                rhs_scale=w_scales[s][:, c0 : c0 + n],
+                lhsT=picked_words[s][:, d, :].bitcast(FP8X4),
+                lhsT_scale=picked_scales[s][:, d, :],
+                rhs=w_codes[s][:, cols].bitcast(FP8X4),
+                rhs_scale=w_scales[s][:, cols],
                 start=True,
                 stop=True,
             )
-            return y[:].rearrange("v (m t) -> v t m", t=PACK)
+            return y[:]
 
-        def turn(f, terms):
-            for a, term in enumerate(terms):
-                for t in range(PACK):
-                    nc.tensor.matmul(
-                        f[:, t, :], term[:, t, :], ident[:], is_transpose=True,
-                        start=(a == 0 and t == 0), stop=(a == len(terms) - 1 and t == PACK - 1),
-                    )
+        def weigh_on_scalar(dst, y, weight):
+            nc.scalar.activation(dst, y, COPY, scale=weight)
 
-        feat = [psum.tile([P, PACK, V], F32, name="feat%d" % s) for s in range(3)]
-        scaled = [[sb([P, PACK, P], F32, "scaled%d_%d" % (s, d)) for d in range(D)] for s in range(3)]
-        pair = [[sb([P, PACK, P], F32, "pair%d_%d" % (s, a)) for a in range(2)] for s in range(3)]
+        def weigh_on_vector(dst, y, weight):
+            nc.vector.tensor_scalar(dst, y, weight, None, MULT)
 
-        def products(s, c0, n, engs="SSSS"):
-            part = slice(c0 // PACK, (c0 + n) // PACK)
+        def weighted_products(s):
             for d in range(D):
-                y = product(s, d, c0, n)
-                if engs[d] == "S":
-                    nc.scalar.activation(scaled[s][d][:, :, part], y, COPY, scale=bl[s][:, d : d + 1])
-                elif engs[d] == "V":
-                    nc.vector.tensor_scalar(scaled[s][d][:, :, part], y, bl[s][:, d : d + 1], None, MULT)
-                else:
-                    nc.vector.scalar_tensor_tensor(
-                        pair[s][d // 2][:, :, part], y, bl[s][:, d : d + 1], scaled[s][d - 1][:, :, part], MULT, ADD
-                    )
+                y = product(s, d, slice(0, H))
+                weigh_on_scalar(weighted[s][d][:], y.rearrange("v (m t) -> v t m", t=SLOTS), bilinear[s][:, d : d + 1])
 
-        f0 = sb([P, V, PACK], F32, "f0")
+        def weighted_products_of_w3_half(h, weigh):
+            for d in range(D):
+                y = product(LAST, d, halves[h])
+                dst = weighted[LAST][d][:, 2 * h : 2 * h + 2, :].rearrange("v t m -> v (t m)")
+                weigh[d](dst, y, bilinear[LAST][:, d : d + 1])
+
+        def sum_corners(s, order):
+            for n, (d, t) in enumerate(order):
+                nc.tensor.matmul(
+                    feature[s][:, t, :],
+                    weighted[s][d][:, t, :],
+                    identity[:],
+                    is_transpose=True,
+                    start=(n == 0),
+                    stop=(n == len(order) - 1),
+                )
+
+        def slots_side_by_side(bank):
+            return bank[:].rearrange("p t v -> p v t")
+
+        by_corner = [(d, t) for d in range(D) for t in range(SLOTS)]
+        by_half_then_corner = [(d, t) for h in range(2) for d in range(D) for t in (2 * h, 2 * h + 1)]
 
         gather_scales(0)
         deal_scales(0)
         gather_words(0)
-        cast_w("S", 0, 0, 256)
-        cast_w("S", 0, 256, 256)
+        round_weight_half(nc.scalar.copy, 0, 0)
+        round_weight_half(nc.scalar.copy, 0, 1)
         gather_scales(1)
         deal_scales(1)
-        quant_w(0, 0, 512)
-        cast_w("S", 1, 0, 256)
-        products(0, 0, 512)
-        gather_words(1)
-        cast_w("V", 1, 256, 256)
-        quant_w(1, 0, 512)
-        products(1, 0, 512)
-        gather_scales(2)
-        gather_words(2)
-        deal_scales(2)
-        cast_w("V", 2, 0, 256)
-        cast_w("V", 2, 256, 256)
-        quant_w(2, 0, 512)
-        turn(feat[0], scaled[0])
-        nc.scalar.copy(f0[:], feat[0][:].rearrange("p t v -> p v t"))
-        turn(feat[1], scaled[1])
-        cast("S", w4_grp[:], w4_raw[:])
-        quantize(w4_codes[:], w4_scales[:], w4_grp[:])
-        f01 = sb([P, V, PACK], F32, "f01", "wgrp2")
-        nc.vector.tensor_tensor(f01[:], feat[1][:].rearrange("p t v -> p v t"), f0[:], MULT)
-        products(2, 0, 512, "SVSV")
-        turn(feat[2], scaled[2])
+        quantize_weight(0, slice(0, H))
+        round_weight_half(nc.scalar.copy, 1, 0)
+        weighted_products(0)
 
-        z = sb([P, V, PACK], BF16, "z")
-        z_codes = sb([P, V], U32, "zcodes")
-        z_scales = sb([P, V], U8, "zscales")
-        nc.vector.tensor_tensor(z[:], feat[2][:].rearrange("p t v -> p v t"), f01[:], MULT)
-        quantize(z_codes[:], z_scales[:], z[:])
-        acc = psum.tile([P, V], F32, name="acc")
-        nc.tensor.matmul_mx(
-            out=acc[:], lhsT=w4_codes[:].bitcast(FP8X4), lhsT_scale=w4_scales[:],
-            rhs=z_codes[:].bitcast(FP8X4), rhs_scale=z_scales[:], start=True, stop=True,
-        )
-        result = sb([P, V], F32, "result")
-        nc.scalar.activation(result[:], acc[:], SIGMOID)
+        gather_words(1)
+        round_weight_half(nc.vector.tensor_copy, 1, 1)
+        quantize_weight(1, slice(0, H))
+        weighted_products(1)
+
+        gather_scales(LAST)
+        gather_words(LAST)
+        deal_scales(LAST)
+        for h in range(2):
+            round_w3_half(h)
+        for h in range(2):
+            quantize_weight(LAST, halves[h])
+
+        f0 = sbuf([P, V, SLOTS], F32, "f0")
+        sum_corners(0, by_corner)
+        nc.scalar.copy(f0[:], slots_side_by_side(feature[0]))
+        sum_corners(1, by_corner)
+        round_columns(nc.scalar.copy, w4_rounded[:], w4_raw[:])
+
+        weighted_products_of_w3_half(0, [weigh_on_scalar] * D)
+        quantize(w4_codes[:], w4_scales[:], w4_rounded[:])
+        f01 = sbuf([P, V, SLOTS], F32, "f01", tag="w_rounded%d" % LAST)
+        nc.vector.tensor_tensor(f01[:], slots_side_by_side(feature[1]), f0[:], MULT)
+        weighted_products_of_w3_half(1, [weigh_on_vector, weigh_on_scalar, weigh_on_vector, weigh_on_vector])
+        sum_corners(LAST, by_half_then_corner)
+
+        z = sbuf([P, V, SLOTS], BF16, "z")
+        z_codes = sbuf([P, V], U32, "z_codes")
+        z_scales = sbuf([P, V], U8, "z_scales")
+        result = sbuf([P, V], F32, "result")
+        sample_halves = (slice(0, V // 2), slice(V // 2, V))
+        for vs in sample_halves:
+            nc.vector.tensor_tensor(z[:, vs, :], slots_side_by_side(feature[LAST])[:, vs, :], f01[:, vs, :], MULT)
+        for vs in sample_halves:
+            quantize(z_codes[:, vs], z_scales[:, vs], z[:, vs, :])
+        for vs in sample_halves:
+            logits = product_banks.tile([P, V // 2], F32, name="logits", tag="product")
+            nc.tensor.matmul_mx(
+                out=logits[:],
+                lhsT=w4_codes[:].bitcast(FP8X4),
+                lhsT_scale=w4_scales[:],
+                rhs=z_codes[:, vs].bitcast(FP8X4),
+                rhs_scale=z_scales[:, vs],
+                start=True,
+                stop=True,
+            )
+            nc.scalar.activation(result[:, vs], logits[:], SIGMOID)
         nc.sync.dma_start(out, result[:])

from contextlib import ExitStack

import concourse.mybir as mybir
from concourse.masks import make_identity

K, T, S, D, H, N = 512, 1024, 512, 4, 512, 128
FLOPS = 2 * (3 * K * H * S + H * N * (S // D))

F32 = mybir.dt.float32
BF16 = mybir.dt.bfloat16
I32 = mybir.dt.int32
U32 = mybir.dt.uint32
U16 = mybir.dt.uint16
U8 = mybir.dt.uint8
FP8X4 = mybir.dt.float8_e4m3fn_x4
COPY = mybir.ActivationFunctionType.Copy
SIGMOID = mybir.ActivationFunctionType.Sigmoid
MULT = mybir.AluOpType.mult

P = 128
SLOTS = 4
PLANES = 3
LAST = PLANES - 1
V = S // D
HALF = H // 2
QUADRANT = 32
RUN = 4
PRODUCT_BANKS = 5


def tile_picked_ytripl_sigmoid_p_kernel(
    tc, x_words, x_scales, e_words, e_scales, d_words, d_scales, w1, bl0, w2, bl1, w3, bl2, w4, offs, plb, plc, out
):
    nc = tc.nc
    words_hbm = (x_words, e_words, d_words)
    scales_hbm = (x_scales, e_scales, d_scales)
    lists_hbm = (offs, plb, plc)
    bilinear_hbm = (bl0, bl1, bl2)
    halves = (slice(0, HALF), slice(HALF, H))

    with ExitStack() as ctx:
        keep = ctx.enter_context(tc.tile_pool(name="keep", bufs=1))
        feature_banks = ctx.enter_context(tc.psum_pool(name="feature_banks", bufs=1))
        product_banks = ctx.enter_context(tc.psum_pool(name="product_banks", bufs=PRODUCT_BANKS))

        def sbuf(shape, dtype, name, tag=None):
            return keep.tile(shape, dtype, name=name, tag=tag or name, align_bytes=64)

        def per_plane(shape, dtype, name):
            return [sbuf(shape, dtype, "%s%d" % (name, s)) for s in range(PLANES)]

        lists = per_plane([P, S // 16], U16, "list")
        word_table = per_plane([P, T], I32, "word_table")
        scale_table = per_plane([P, T], U8, "scale_table")
        bilinear = per_plane([P, D], F32, "bilinear")
        w_halves = [[sbuf([P, SLOTS, HALF], F32, "w_raw%d_%d" % (s, h)) for h in range(2)] for s in range(LAST)]
        w3_raw = sbuf([P, SLOTS, H], F32, "w3_raw")
        w4_raw = sbuf([P, SLOTS, N], F32, "w4_raw")
        identity = sbuf([P, P], F32, "identity")

        def load_list(s):
            nc.sync.dma_start(lists[s][:], lists_hbm[s])

        def load_scales(s):
            for q in range(P // QUADRANT):
                nc.sync.dma_start(
                    scale_table[s][QUADRANT * q : QUADRANT * q + 4, :].bitcast(I32),
                    scales_hbm[s][0, 4 * q : 4 * q + 4, :].bitcast(I32),
                )

        def load_words(s):
            nc.sync.dma_start(word_table[s][:], words_hbm[s][0].rearrange("p c j -> p (c j)").bitcast(I32))

        def by_slot(w):
            return w.rearrange("(p j) c -> p j c", j=SLOTS)

        def load_weight_half(s, h):
            nc.sync.dma_start(w_halves[s][h][:], by_slot((w1, w2)[s])[:, :, halves[h]])

        def load_bilinear(s):
            nc.sync.dma_start(bilinear[s][:], bilinear_hbm[s][0].rearrange("(v d) -> v d", d=D))

        for s in range(PLANES):
            nc.gpsimd.memset(scale_table[s][:].bitcast(I32), 0)
        make_identity(nc, identity[:])

        load_list(0)
        load_scales(0)
        load_words(0)
        load_weight_half(0, 0)
        load_list(1)
        load_scales(1)
        load_weight_half(0, 1)
        load_weight_half(1, 0)
        load_bilinear(0)
        load_bilinear(1)
        load_words(1)
        load_weight_half(1, 1)
        load_list(LAST)
        load_words(LAST)
        load_scales(LAST)
        nc.sync.dma_start(w3_raw[:], by_slot(w3))
        nc.sync.dma_start(w4_raw[:], by_slot(w4))
        load_bilinear(LAST)

        picked_words = per_plane([P, D, V], U32, "picked_words")
        listed_scales = per_plane([P, S], U8, "listed_scales")
        picked_scales = per_plane([P, D, V], U8, "picked_scales")

        def gather_words(s):
            nc.vector.tensor_copy(
                picked_words[s][:].rearrange("p d v -> p v d"), word_table[s][:].bitcast(U32).indirect(lists[s][:])
            )

        def gather_scales(s):
            nc.vector.tensor_copy(listed_scales[s][:], scale_table[s][:].indirect(lists[s][:]))

        def deal_scales(s):
            nc.vector.tensor_copy(picked_scales[s][:], listed_scales[s][:].rearrange("p (v d) -> p d v", d=D))

        w_rounded = per_plane([P, H, SLOTS], BF16, "w_rounded")
        w_codes = per_plane([P, H], U32, "w_codes")
        w_scales = per_plane([P, H], U8, "w_scales")
        w4_rounded = sbuf([P, N, SLOTS], BF16, "w4_rounded")
        w4_codes = sbuf([P, N], U32, "w4_codes")
        w4_scales = sbuf([P, N], U8, "w4_scales")

        def round_columns(copy, rounded, raw):
            copy(rounded.rearrange("p (c i) j -> p c j i", i=RUN), raw.rearrange("p j (c i) -> p c j i", i=RUN))

        def round_weight_half(copy, s, h):
            round_columns(copy, w_rounded[s][:, halves[h], :], w_halves[s][h][:])

        def round_w3_half(h):
            ts = slice(2 * h, 2 * h + 2)
            nc.vector.tensor_copy(
                w_rounded[LAST][:].rearrange("p (t m) j -> p m j t", t=SLOTS)[:, :, :, ts],
                w3_raw[:].rearrange("p j (m t) -> p m j t", t=SLOTS)[:, :, :, ts],
            )

        def quantize(codes, scales, rounded):
            nc.vector.quantize_mx(out=codes.bitcast(FP8X4), scales=scales, in_=rounded.rearrange("p c j -> p (c j)"))

        def quantize_weight(s, cols):
            quantize(w_codes[s][:, cols], w_scales[s][:, cols], w_rounded[s][:, cols, :])

        feature = [feature_banks.tile([P, SLOTS, V], F32, name="feature%d" % s) for s in range(PLANES)]
        weighted = [[sbuf([P, SLOTS, P], F32, "weighted%d_%d" % (s, d)) for d in range(D)] for s in range(PLANES)]

        def product(s, d, cols):
            y = product_banks.tile([P, cols.stop - cols.start], F32, name="y", tag="product")
            nc.tensor.matmul_mx(
                out=y[:],
                lhsT=picked_words[s][:, d, :].bitcast(FP8X4),
                lhsT_scale=picked_scales[s][:, d, :],
                rhs=w_codes[s][:, cols].bitcast(FP8X4),
                rhs_scale=w_scales[s][:, cols],
                start=True,
                stop=True,
            )
            return y[:]

        def weigh_on_scalar(dst, y, weight):
            nc.scalar.activation(dst, y, COPY, scale=weight)

        def weigh_on_vector(dst, y, weight):
            nc.vector.tensor_scalar(dst, y, weight, None, MULT)

        def weighted_products(s):
            for d in range(D):
                y = product(s, d, slice(0, H))
                weigh_on_scalar(weighted[s][d][:], y.rearrange("v (m t) -> v t m", t=SLOTS), bilinear[s][:, d : d + 1])

        def weighted_products_of_w3_half(h, weigh):
            for d in range(D):
                y = product(LAST, d, halves[h])
                dst = weighted[LAST][d][:, 2 * h : 2 * h + 2, :].rearrange("v t m -> v (t m)")
                weigh[d](dst, y, bilinear[LAST][:, d : d + 1])

        def sum_corners(s, order):
            for n, (d, t) in enumerate(order):
                nc.tensor.matmul(
                    feature[s][:, t, :],
                    weighted[s][d][:, t, :],
                    identity[:],
                    is_transpose=True,
                    start=(n == 0),
                    stop=(n == len(order) - 1),
                )

        def slots_side_by_side(bank):
            return bank[:].rearrange("p t v -> p v t")

        by_corner = [(d, t) for d in range(D) for t in range(SLOTS)]
        by_half_then_corner = [(d, t) for h in range(2) for d in range(D) for t in (2 * h, 2 * h + 1)]

        gather_scales(0)
        deal_scales(0)
        gather_words(0)
        round_weight_half(nc.scalar.copy, 0, 0)
        round_weight_half(nc.scalar.copy, 0, 1)
        gather_scales(1)
        deal_scales(1)
        quantize_weight(0, slice(0, H))
        round_weight_half(nc.scalar.copy, 1, 0)
        weighted_products(0)

        gather_words(1)
        round_weight_half(nc.vector.tensor_copy, 1, 1)
        quantize_weight(1, slice(0, H))
        weighted_products(1)

        gather_scales(LAST)
        gather_words(LAST)
        deal_scales(LAST)
        for h in range(2):
            round_w3_half(h)
        for h in range(2):
            quantize_weight(LAST, halves[h])

        f0 = sbuf([P, V, SLOTS], F32, "f0")
        sum_corners(0, by_corner)
        nc.scalar.copy(f0[:], slots_side_by_side(feature[0]))
        sum_corners(1, by_corner)
        round_columns(nc.scalar.copy, w4_rounded[:], w4_raw[:])

        weighted_products_of_w3_half(0, [weigh_on_scalar] * D)
        quantize(w4_codes[:], w4_scales[:], w4_rounded[:])
        f01 = sbuf([P, V, SLOTS], F32, "f01", tag="w_rounded%d" % LAST)
        nc.vector.tensor_tensor(f01[:], slots_side_by_side(feature[1]), f0[:], MULT)
        weighted_products_of_w3_half(1, [weigh_on_vector, weigh_on_scalar, weigh_on_vector, weigh_on_vector])
        sum_corners(LAST, by_half_then_corner)

        z = sbuf([P, V, SLOTS], BF16, "z")
        z_codes = sbuf([P, V], U32, "z_codes")
        z_scales = sbuf([P, V], U8, "z_scales")
        result = sbuf([P, V], F32, "result")
        sample_halves = (slice(0, V // 2), slice(V // 2, V))
        for vs in sample_halves:
            nc.vector.tensor_tensor(z[:, vs, :], slots_side_by_side(feature[LAST])[:, vs, :], f01[:, vs, :], MULT)
        for vs in sample_halves:
            quantize(z_codes[:, vs], z_scales[:, vs], z[:, vs, :])
        for vs in sample_halves:
            logits = product_banks.tile([P, V // 2], F32, name="logits", tag="product")
            nc.tensor.matmul_mx(
                out=logits[:],
                lhsT=w4_codes[:].bitcast(FP8X4),
                lhsT_scale=w4_scales[:],
                rhs=z_codes[:, vs].bitcast(FP8X4),
                rhs_scale=z_scales[:, vs],
                start=True,
                stop=True,
            )
            nc.scalar.activation(result[:, vs], logits[:], SIGMOID)
        nc.sync.dma_start(out, result[:])
